import numpy as np
import ml_dtypes


def mxq(x, axis, fmt="e4m3"):
    dtype, down = {"e4m3": (ml_dtypes.float8_e4m3fn, 7), "e5m2": (ml_dtypes.float8_e5m2, 14)}[fmt]
    v = np.moveaxis(np.asarray(x, np.float32).astype(ml_dtypes.bfloat16).astype(np.float64), axis, -1)
    blocks = v.reshape(v.shape[:-1] + (-1, 32))
    amax = np.abs(blocks).max(-1, keepdims=True)
    byte = np.maximum(np.where(amax > 0, np.frexp(amax)[1] - 1 + 127, 0) - down, 1)
    scale = np.exp2(byte - 127.0)
    codes = (blocks / scale).astype(np.float32).astype(dtype).astype(np.float64)
    return np.moveaxis((codes * scale).reshape(v.shape), -1, axis)


WIDE = False


def mx_kscale(k):
    if not WIDE:
        return np.ones(k)
    levels = np.array([10, -10, 5, -5, 0])
    if k % 512:
        return np.exp2(np.random.permutation(np.resize(levels, k // 32))).repeat(32)
    a = np.empty((k // 512, 16))
    for p in range(k // 512):
        a[p, :8] = np.random.permutation(np.resize(levels, 8))
        for g in range(8):
            far = levels[np.abs(levels - a[p, g]) >= 10]
            a[p, g + 8] = far[np.random.randint(len(far))]
    return np.exp2(a.ravel()).repeat(32)


def f64(x):
    return np.asarray(x).astype(np.float64)


def striped(idx):
    return np.tile(idx.reshape(-1, 16).T, (8, 1)).astype(np.uint16)


def unstriped(offs):
    return offs[:16].T.reshape(-1).astype(np.int64)


E2M1 = np.array([0.0, 0.5, 1.0, 1.5, 2.0, 3.0, 4.0, 6.0, -0.0, -0.5, -1.0, -1.5, -2.0, -3.0, -4.0, -6.0])


def pack_weight(w, fmt):
    k, n = w.shape
    w = f64(np.asarray(w, np.float32).astype(ml_dtypes.bfloat16)).reshape(k // 32, 32, n)
    amax = np.abs(w).max(1)
    if fmt == "e4m3":
        byte = np.frexp(amax)[1] - 1 + 127 - 7
    else:
        mant, ex = np.frexp(amax / 6.0)
        byte = np.where(mant > 0.5, ex, ex - 1) + 127
    byte = np.clip(np.where(amax > 0, byte, 1), 1, 254)
    scaled = (w * np.exp2(127.0 - byte)[:, None, :]).reshape(k, n).astype(np.float32)
    by_word = np.ascontiguousarray(scaled.reshape(k // 512, 128, 4, n).transpose(0, 1, 3, 2))
    if fmt == "e4m3":
        words = by_word.astype(ml_dtypes.float8_e4m3fn).view(np.uint8)
    else:
        c = by_word.astype(ml_dtypes.float4_e2m1fn).view(np.uint8) & 0xF
        words = (c[..., 0::2] | (c[..., 1::2] << 4)).reshape(k // 512, 128, 2 * n)
    return np.ascontiguousarray(words), np.ascontiguousarray(byte.astype(np.uint8).reshape(k // 512, 16, n))


def unpack_weight(words, scales, fmt):
    g, _, n = scales.shape
    words = np.ascontiguousarray(words).reshape(g, 128, n, -1)
    if fmt == "e4m3":
        vals = words.view(ml_dtypes.float8_e4m3fn).astype(np.float64)
    else:
        nib = np.empty((g, 128, n, 4), np.uint8)
        nib[..., 0::2] = words & 0xF
        nib[..., 1::2] = words >> 4
        vals = E2M1[nib]
    vals = vals * np.repeat(np.exp2(scales.astype(np.float64) - 127.0), 8, axis=1)[..., None]
    return vals.transpose(0, 1, 3, 2).reshape(g * 512, n)


def gelu(v):
    return 0.5 * v * (1.0 + np.tanh(np.sqrt(2.0 / np.pi) * (v + 0.044715 * v**3)))


K, T, S, P, H = 1024, 4096, 1024, 512, 512

def setup_inputs():
    n = np.random.standard_normal
    s = mx_kscale(K)[:, None]
    u = mx_kscale(H)[:, None]
    tab_words, tab_scales = pack_weight(n((K, T)) * s, "e4m3")
    w3_words, w3_scales = pack_weight(n((K, H)) / np.sqrt(K) / s * u.T, "e2m1")
    return {
        "tab_words": tab_words, "tab_scales": tab_scales,
        "offs": striped(np.random.permutation(T)[:S]),
        "pos1": striped(np.random.permutation(S)[:P]),
        "w1": (1.2 * n((K, H)) / np.sqrt(K) / s * u.T).astype(np.float32),
        "w2": (0.5 * n((K, H)) / np.sqrt(K) / s).astype(np.float32),
        "w3_words": w3_words, "w3_scales": w3_scales,
        "gain": np.exp(0.4 * n(H)).astype(np.float32),
        "splice": (0.8 * n((H, P)) * u).astype(np.float32),
        "w4": (n((H, H)) / np.sqrt(H) / u).astype(np.float32),
        "skip": (np.exp(0.3 * n(H)) / u[:, 0]).astype(np.float32),
        "wgo": np.exp(0.3 * n((128, P))).astype(np.float32),
    }

def reference(tab_words, tab_scales, offs, pos1, w1, w2, w3_words, w3_scales, gain, splice, w4, skip, wgo):
    v = unpack_weight(tab_words, tab_scales, "e4m3")[:, unstriped(offs)]
    a = mxq(f64(w1), 0, "e4m3").T @ v
    b = mxq(f64(w2), 0, "e4m3").T @ v
    d = unpack_weight(w3_words, w3_scales, "e2m1").T @ v
    h = f64(gain)[:, None] * np.maximum(a * np.cos(b), d)
    x = mxq(h[:, unstriped(pos1)] + f64(splice), 0, "e4m3")
    y = np.tanh(mxq(f64(w4), 0, "e4m3").T @ x)
    out = f64(skip)[:, None] * h
    out[:, unstriped(pos1)] = np.tile(f64(wgo), (H // 128, 1)) * y
    return out

@@ -1,0 +1,274 @@
+import math
+from contextlib import ExitStack
+
+import concourse.mybir as mybir
+
+K, T, S, M, H = 1024, 4096, 1024, 512, 512
+FLOPS = 2 * (3 * K * H * S + H * H * M)
+
+F32 = mybir.dt.float32
+BF16 = mybir.dt.bfloat16
+I32 = mybir.dt.int32
+U32 = mybir.dt.uint32
+U16 = mybir.dt.uint16
+U8 = mybir.dt.uint8
+FP8X4 = mybir.dt.float8_e4m3fn_x4
+FP4X4 = mybir.dt.float4_e2m1fn_x4
+ACT = mybir.ActivationFunctionType
+ALU = mybir.AluOpType
+
+P = 128
+PACK = 4
+K_PASS = P * PACK
+PASSES = K // K_PASS
+BANK = 512
+UNITS = S // BANK
+CHUNK = 256
+CHUNKS = M // CHUNK
+
+
+def tile_list_torn_strip_splice_kernel(
+    tc, tab_words, tab_scales, offs, pos1, w1, w2, w3_words, w3_scales, gain, splice, w4, skip, wgo, out
+):
+    nc = tc.nc
+    with ExitStack() as ctx:
+        lists = ctx.enter_context(tc.tile_pool(name="lists", bufs=1))
+        keep = ctx.enter_context(tc.tile_pool(name="keep", bufs=1))
+        ring = ctx.enter_context(tc.tile_pool(name="ring", bufs=3))
+        psum = ctx.enter_context(tc.psum_pool(name="psum", bufs=1))
+
+        offs_sb = lists.tile([P, S // 16], U16, name="offs_sb")
+        pos_sb = lists.tile([P, M // 16], U16, name="pos_sb")
+
+        tab_s = keep.tile([P, T], U8, name="tab_s", align_bytes=64)
+        v_s = keep.tile([P, S], U8, name="v_s", align_bytes=64)
+        planes = keep.tile([P, PASSES * S], U8, name="planes", align_bytes=64)
+        w3_s_raw = keep.tile([P, PASSES, H], U8, name="w3_s_raw", align_bytes=64)
+        nc.vector.memset(tab_s[32:64, :].bitcast(I32), 0)
+        nc.vector.memset(tab_s[64:128, :].bitcast(I32), 0)
+        nc.gpsimd.memset(w3_s_raw[:].rearrange("p a c -> p (a c)").bitcast(I32), 0)
+        nc.gpsimd.memset(planes[:].bitcast(I32), 0)
+
+        tab_w = [keep.tile([P, T], U32, name=f"tab_w{a}", align_bytes=64) for a in range(PASSES)]
+        v_w = [keep.tile([P, S], U32, name=f"v_w{a}", align_bytes=64) for a in range(PASSES)]
+
+        def load_table_words(a):
+            nc.sync.dma_start(
+                out=tab_w[a][:].bitcast(I32),
+                in_=tab_words[a].rearrange("p t i -> p (t i)").bitcast(I32),
+            )
+
+        def load_rows(name, rows, pieces=1):
+            width = H // pieces
+            parts = []
+            for i in range(pieces):
+                raw = keep.tile([P, PACK, width], F32, name=f"{name}_raw{i}")
+                nc.sync.dma_start(
+                    out=raw[:],
+                    in_=rows[:, i * width : (i + 1) * width].rearrange("(p j) c -> p j c", j=PACK),
+                )
+                parts.append(raw)
+            return parts
+
+        nc.sync.dma_start(offs_sb[:], offs)
+        nc.sync.dma_start(
+            out=tab_s[0:32, :].bitcast(I32), in_=tab_scales.rearrange("a q t -> (a q) t").bitcast(I32)
+        )
+        load_table_words(0)
+        load_table_words(1)
+        w3_w_raw = keep.tile([P, PASSES, 2 * H], U8, name="w3_w_raw", align_bytes=64)
+        nc.sync.dma_start(
+            out=w3_w_raw[:].bitcast(I32), in_=w3_words.rearrange("a p c -> p a c").bitcast(I32)
+        )
+        w2_raw = [load_rows(f"w2_{a}", w2[a * K_PASS : (a + 1) * K_PASS, :]) for a in range(PASSES)]
+        w1_raw = [
+            load_rows(f"w1_{a}", w1[a * K_PASS : (a + 1) * K_PASS, :], pieces=1 + a) for a in range(PASSES)
+        ]
+        gain_sb = keep.tile([P, PACK], F32, name="gain_sb")
+        skip_sb = keep.tile([P, PACK], F32, name="skip_sb")
+        nc.sync.dma_start(out=gain_sb[:], in_=gain.rearrange("(p t) -> p t", t=PACK))
+        nc.sync.dma_start(out=skip_sb[:], in_=skip.rearrange("(p t) -> p t", t=PACK))
+        splice_sb = load_rows("splice", splice)[0]
+        nc.sync.dma_start(pos_sb[:], pos1)
+        w4_raw = load_rows("w4", w4)
+        wgo_sb = keep.tile([P, PACK * M], F32, name="wgo_sb")
+        for q in range(4):
+            nc.sync.dma_start(
+                out=wgo_sb[32 * q : 32 * q + 32, :], in_=wgo.rearrange("(r t) m -> r (t m)", t=PACK)
+            )
+
+        for q in range(4):
+            nc.gpsimd.dma_start(
+                out=w3_s_raw[32 * q : 32 * q + 4, :, :].bitcast(I32),
+                in_=w3_scales[:, 4 * q : 4 * q + 4, :].rearrange("a r c -> r a c").bitcast(I32),
+            )
+
+        nc.vector.tensor_copy(v_s[:], tab_s[:].indirect(offs_sb[:]))
+        for a in range(PASSES):
+            for q in range(4):
+                nc.gpsimd.dma_start(
+                    out=planes[32 * q : 32 * q + 4, a * S : (a + 1) * S].bitcast(I32),
+                    in_=v_s[16 * a + 4 * q : 16 * a + 4 * q + 4, :].bitcast(I32),
+                )
+        nc.vector.tensor_copy(v_w[0][:], tab_w[0][:].indirect(offs_sb[:]))
+        nc.vector.tensor_copy(v_w[1][:], tab_w[1][:].indirect(offs_sb[:]))
+
+        w3_w = keep.tile([P, PASSES * 2 * H], U8, name="w3_w", align_bytes=64)
+        w3_s = keep.tile([P, PASSES * H], U8, name="w3_s", align_bytes=64)
+        nc.vector.tensor_copy(
+            out=w3_w[:].bitcast(U16).rearrange("p (a t m) -> p a m t", a=PASSES, t=PACK),
+            in_=w3_w_raw[:].bitcast(U16).rearrange("p a (m t) -> p a m t", t=PACK),
+        )
+        nc.vector.tensor_copy(
+            out=w3_s[:].rearrange("p (a t m) -> p a m t", a=PASSES, t=PACK),
+            in_=w3_s_raw[:].rearrange("p a (m t) -> p a m t", t=PACK),
+        )
+
+        def round_weights(name, parts, copy):
+            grouped = keep.tile([P, PACK * H], BF16, name=f"{name}_bf", align_bytes=64)
+            dst = grouped[:].rearrange("p (t m j) -> p m t j", t=PACK, j=PACK)
+            ms = P // len(parts)
+            for i, raw in enumerate(parts):
+                copy(out=dst[:, i * ms : (i + 1) * ms], in_=raw[:].rearrange("p j (m t) -> p m t j", t=PACK))
+            return grouped
+
+        def quantise(name, grouped):
+            width = grouped.shape[1] // PACK
+            codes = keep.tile([P, width], U32, name=f"{name}_codes", align_bytes=64)
+            scales = keep.tile([P, width], U8, name=f"{name}_scales", align_bytes=64)
+            nc.vector.quantize_mx(out=codes[:].bitcast(FP8X4), scales=scales[:], in_=grouped[:])
+            return codes, scales
+
+        w2_q = []
+        for a, copy in enumerate((nc.scalar.copy, nc.vector.tensor_copy)):
+            w2_q.append(quantise(f"w2_{a}", round_weights(f"w2_{a}", w2_raw[a], copy)))
+
+        def table_product(acc, weights, t, u):
+            cols = slice(u * BANK, (u + 1) * BANK)
+            rows = slice(t * P, (t + 1) * P)
+            for a in range(PASSES):
+                codes, scales = weights[a]
+                nc.tensor.matmul_mx(
+                    out=acc[:],
+                    lhsT=codes[:, rows].bitcast(FP8X4),
+                    lhsT_scale=scales[:, rows],
+                    rhs=v_w[a][:, cols].bitcast(FP8X4),
+                    rhs_scale=planes[:, a * S + u * BANK : a * S + (u + 1) * BANK],
+                    start=(a == 0),
+                    stop=(a == PASSES - 1),
+                )
+
+        def table_product_fp4(acc, t, u):
+            cols = slice(u * BANK, (u + 1) * BANK)
+            for a in range(PASSES):
+                c0 = a * H + t * P
+                nc.tensor.matmul_mx(
+                    out=acc[:],
+                    lhsT=w3_w[:, 2 * c0 : 2 * (c0 + P)].bitcast(FP4X4),
+                    lhsT_scale=w3_s[:, c0 : c0 + P],
+                    rhs=v_w[a][:, cols].bitcast(FP8X4),
+                    rhs_scale=planes[:, a * S + u * BANK : a * S + (u + 1) * BANK],
+                    start=(a == 0),
+                    stop=(a == PASSES - 1),
+                )
+
+        versine = [keep.tile([P, S], F32, name=f"versine{t}") for t in range(PACK)]
+        for t in range(PACK):
+            for u in range(UNITS):
+                cols = slice(u * BANK, (u + 1) * BANK)
+                b_ps = psum.tile([P, BANK], F32, name="b_ps", bufs=2)
+                table_product(b_ps, w2_q, t, u)
+                half_sine = ring.tile([P, BANK], F32, name="half_sine")
+                nc.scalar.activation(half_sine[:], b_ps[:], ACT.Sin, scale=0.5)
+                nc.scalar.activation(versine[t][:, cols], half_sine[:], ACT.Square, scale=math.sqrt(2.0))
+
+        w1_q = [
+            quantise(f"w1_{a}", round_weights(f"w1_{a}", w1_raw[a], nc.vector.tensor_copy)) for a in range(PASSES)
+        ]
+
+        h = [keep.tile([P, S], F32, name=f"h{t}") for t in range(PACK)]
+        o = [keep.tile([P, S], F32, name=f"o{t}") for t in range(PACK)]
+        x32 = [keep.tile([P, PACK, CHUNK], F32, name=f"x32_{c}") for c in range(CHUNKS)]
+
+        def pick(t, c):
+            nc.vector.tensor_tensor(
+                x32[c][:, t, :],
+                h[t][:].indirect(pos_sb[:, c * CHUNK // 16 : (c + 1) * CHUNK // 16]),
+                splice_sb[:, t, c * CHUNK : (c + 1) * CHUNK],
+                ALU.add,
+            )
+
+        for t in range(PACK):
+            for u in range(UNITS):
+                cols = slice(u * BANK, (u + 1) * BANK)
+                d_ps = psum.tile([P, BANK], F32, name="d_ps", bufs=3)
+                a_ps = psum.tile([P, BANK], F32, name="a_ps", bufs=3)
+                table_product_fp4(d_ps, t, u)
+                table_product(a_ps, w1_q, t, u)
+                minus_ac = ring.tile([P, BANK], F32, name="minus_ac")
+                nc.vector.scalar_tensor_tensor(
+                    minus_ac[:], versine[t][:, cols], 1.0, a_ps[:], ALU.subtract, ALU.mult
+                )
+                larger = ring.tile([P, BANK], F32, name="larger")
+                nc.vector.scalar_tensor_tensor(larger[:], minus_ac[:], -1.0, d_ps[:], ALU.mult, ALU.max)
+                nc.scalar.activation(h[t][:, cols], larger[:], ACT.Copy, scale=gain_sb[:, t : t + 1])
+            if t > 0:
+                pick(t - 1, 0)
+            if t == 1:
+                w4_q = quantise("w4", round_weights("w4", w4_raw, nc.scalar.copy))
+        pick(PACK - 1, 0)
+
+        def interleave(c):
+            x_bf = keep.tile([P, CHUNK * PACK], BF16, name=f"x_bf{c}", align_bytes=64)
+            nc.scalar.copy(
+                out=x_bf[:].rearrange("p (g i t) -> p g t i", i=4, t=PACK),
+                in_=x32[c][:].rearrange("p t (g i) -> p g t i", i=4),
+            )
+            return x_bf
+
+        def second_stage(c, x_q):
+            ys = []
+            for t in range(PACK):
+                rows = slice(t * P, (t + 1) * P)
+                y_ps = psum.tile([P, BANK], F32, name="b_ps", bufs=2)
+                nc.tensor.matmul_mx(
+                    out=y_ps[:, :CHUNK],
+                    lhsT=w4_q[0][:, rows].bitcast(FP8X4),
+                    lhsT_scale=w4_q[1][:, rows],
+                    rhs=x_q[0][:].bitcast(FP8X4),
+                    rhs_scale=x_q[1][:],
+                    start=True,
+                    stop=True,
+                )
+                y = keep.tile([P, CHUNK], F32, name=f"y{c}_{t}")
+                nc.scalar.activation(y[:], y_ps[:, :CHUNK], ACT.Tanh)
+                ys.append(y)
+            return ys
+
+        def put(t, c, y):
+            nc.vector.tensor_tensor(
+                o[t][:].indirect(pos_sb[:, c * CHUNK // 16 : (c + 1) * CHUNK // 16]),
+                y[:],
+                wgo_sb[:, t * M + c * CHUNK : t * M + (c + 1) * CHUNK],
+                ALU.mult,
+            )
+
+        x_bf0 = interleave(0)
+        for t in range(2):
+            pick(t, 1)
+        x_q0 = quantise("x0", x_bf0)
+        for t in range(2, PACK):
+            pick(t, 1)
+        for t in range(PACK):
+            nc.scalar.activation(o[t][:], h[t][:], ACT.Copy, scale=skip_sb[:, t : t + 1])
+        y0 = second_stage(0, x_q0)
+        x_bf1 = interleave(1)
+        put(0, 0, y0[0])
+        x_q1 = quantise("x1", x_bf1)
+        y1 = second_stage(1, x_q1)
+        for t in range(1, PACK):
+            put(t, 0, y0[t])
+        out_rows = out.rearrange("(p t) j -> p t j", t=PACK)
+        for t in range(PACK):
+            put(t, 1, y1[t])
+            nc.sync.dma_start(out=out_rows[:, t, :], in_=o[t][:])

@@ -23,6 +23,8 @@ K_PASS = P * PACK
 PASSES = K // K_PASS
 BANK = 512
 UNITS = S // BANK
+RUN = 8
+BLOCKS = H // 32
 CHUNK = 256
 CHUNKS = M // CHUNK
 
@@ -70,32 +72,47 @@ def tile_list_torn_strip_splice_kernel(
                 parts.append(raw)
             return parts
 
+        def dealt(rows):
+            return rows.rearrange("(b t q) c -> t b q c", t=PACK, q=RUN)
+
+        def load_dealt(name, rows):
+            slots = keep.tile([P, PACK, rows.shape[1]], F32, name=name)
+            for t in range(PACK):
+                nc.sync.dma_start(out=slots[:, t, :], in_=dealt(rows)[t])
+            return slots
+
+        def load_factors(name, vec):
+            columns = []
+            for t in range(PACK):
+                column = keep.tile([P, 1], F32, name=f"{name}{t}")
+                nc.sync.dma_start(out=column[:], in_=dealt(vec.unsqueeze(1))[t], allow_slow_non_contiguous=True)
+                columns.append(column)
+            return columns
+
         nc.sync.dma_start(offs_sb[:], offs)
         nc.sync.dma_start(
             out=tab_s[0:32, :].bitcast(I32), in_=tab_scales.rearrange("a q t -> (a q) t").bitcast(I32)
         )
         load_table_words(0)
+        w2_raw = [load_rows(f"w2_{a}", w2[a * K_PASS : (a + 1) * K_PASS, :]) for a in range(PASSES)]
         load_table_words(1)
         w3_w_raw = keep.tile([P, PASSES, 2 * H], U8, name="w3_w_raw", align_bytes=64)
         nc.sync.dma_start(
             out=w3_w_raw[:].bitcast(I32), in_=w3_words.rearrange("a p c -> p a c").bitcast(I32)
         )
-        w2_raw = [load_rows(f"w2_{a}", w2[a * K_PASS : (a + 1) * K_PASS, :]) for a in range(PASSES)]
         w1_raw = [
             load_rows(f"w1_{a}", w1[a * K_PASS : (a + 1) * K_PASS, :], pieces=1 + a) for a in range(PASSES)
         ]
-        gain_sb = keep.tile([P, PACK], F32, name="gain_sb")
-        skip_sb = keep.tile([P, PACK], F32, name="skip_sb")
-        nc.sync.dma_start(out=gain_sb[:], in_=gain.rearrange("(p t) -> p t", t=PACK))
-        nc.sync.dma_start(out=skip_sb[:], in_=skip.rearrange("(p t) -> p t", t=PACK))
-        splice_sb = load_rows("splice", splice)[0]
+        w4_raw = load_dealt("w4_raw", w4)
+        gain_sb = load_factors("gain", gain)
         nc.sync.dma_start(pos_sb[:], pos1)
-        w4_raw = load_rows("w4", w4)
+        splice_sb = load_dealt("splice_sb", splice)
+        skip_sb = load_factors("skip", skip)
         wgo_sb = keep.tile([P, PACK * M], F32, name="wgo_sb")
-        for q in range(4):
-            nc.sync.dma_start(
-                out=wgo_sb[32 * q : 32 * q + 32, :], in_=wgo.rearrange("(r t) m -> r (t m)", t=PACK)
-            )
+        for t in range(PACK):
+            nc.sync.dma_start(out=wgo_sb[0:32, t * M : (t + 1) * M], in_=dealt(wgo)[t])
+        for q in range(1, 4):
+            nc.sync.dma_start(out=wgo_sb[32 * q : 32 * q + 32, :], in_=wgo_sb[0:32, :])
 
         for q in range(4):
             nc.gpsimd.dma_start(
@@ -111,37 +128,48 @@ def tile_list_torn_strip_splice_kernel(
                     in_=v_s[16 * a + 4 * q : 16 * a + 4 * q + 4, :].bitcast(I32),
                 )
         nc.vector.tensor_copy(v_w[0][:], tab_w[0][:].indirect(offs_sb[:]))
-        nc.vector.tensor_copy(v_w[1][:], tab_w[1][:].indirect(offs_sb[:]))
-
         w3_w = keep.tile([P, PASSES * 2 * H], U8, name="w3_w", align_bytes=64)
         w3_s = keep.tile([P, PASSES * H], U8, name="w3_s", align_bytes=64)
-        nc.vector.tensor_copy(
-            out=w3_w[:].bitcast(U16).rearrange("p (a t m) -> p a m t", a=PASSES, t=PACK),
-            in_=w3_w_raw[:].bitcast(U16).rearrange("p a (m t) -> p a m t", t=PACK),
-        )
-        nc.vector.tensor_copy(
-            out=w3_s[:].rearrange("p (a t m) -> p a m t", a=PASSES, t=PACK),
-            in_=w3_s_raw[:].rearrange("p a (m t) -> p a m t", t=PACK),
-        )
+
+        def deal_bytes(dst, src):
+            nc.vector.tensor_copy(
+                out=dst[:].bitcast(I32).rearrange("p (a t b w) -> p a t b w", a=PASSES, t=PACK, b=BLOCKS),
+                in_=src[:].bitcast(I32).rearrange("p a (b t w) -> p a t b w", t=PACK, b=BLOCKS),
+            )
+
+        deal_bytes(w3_s, w3_s_raw)
 
         def round_weights(name, parts, copy):
             grouped = keep.tile([P, PACK * H], BF16, name=f"{name}_bf", align_bytes=64)
-            dst = grouped[:].rearrange("p (t m j) -> p m t j", t=PACK, j=PACK)
-            ms = P // len(parts)
+            dst = grouped[:].rearrange("p (t b q j) -> p t b q j", t=PACK, q=RUN, j=PACK)
+            bs = BLOCKS // len(parts)
             for i, raw in enumerate(parts):
-                copy(out=dst[:, i * ms : (i + 1) * ms], in_=raw[:].rearrange("p j (m t) -> p m t j", t=PACK))
+                copy(
+                    out=dst[:, :, i * bs : (i + 1) * bs],
+                    in_=raw[:].rearrange("p j (b t q) -> p t b q j", t=PACK, q=RUN),
+                )
             return grouped
 
-        def quantise(name, grouped):
+        def quantise(name, grouped, pieces=1):
             width = grouped.shape[1] // PACK
             codes = keep.tile([P, width], U32, name=f"{name}_codes", align_bytes=64)
             scales = keep.tile([P, width], U8, name=f"{name}_scales", align_bytes=64)
-            nc.vector.quantize_mx(out=codes[:].bitcast(FP8X4), scales=scales[:], in_=grouped[:])
+            step = width // pieces
+            for c0 in range(0, width, step):
+                nc.vector.quantize_mx(
+                    out=codes[:, c0 : c0 + step].bitcast(FP8X4),
+                    scales=scales[:, c0 : c0 + step],
+                    in_=grouped[:, PACK * c0 : PACK * (c0 + step)],
+                )
             return codes, scales
 
-        w2_q = []
-        for a, copy in enumerate((nc.scalar.copy, nc.vector.tensor_copy)):
-            w2_q.append(quantise(f"w2_{a}", round_weights(f"w2_{a}", w2_raw[a], copy)))
+        w2_q = [quantise(f"w2_{a}", round_weights(f"w2_{a}", w2_raw[a], nc.vector.tensor_copy)) for a in range(PASSES)]
+        for u in range(UNITS):
+            nc.vector.tensor_copy(
+                v_w[1][:, u * BANK : (u + 1) * BANK],
+                tab_w[1][:].indirect(offs_sb[:, u * BANK // 16 : (u + 1) * BANK // 16]),
+            )
+        deal_bytes(w3_w, w3_w_raw)
 
         def table_product(acc, weights, t, u):
             cols = slice(u * BANK, (u + 1) * BANK)
@@ -172,18 +200,22 @@ def tile_list_torn_strip_splice_kernel(
                     stop=(a == PASSES - 1),
                 )
 
-        versine = [keep.tile([P, S], F32, name=f"versine{t}") for t in range(PACK)]
-        for t in range(PACK):
+        work = [keep.tile([P, S], F32, name=f"work{t}") for t in range(PACK)]
+
+        def versine(t):
             for u in range(UNITS):
                 cols = slice(u * BANK, (u + 1) * BANK)
-                b_ps = psum.tile([P, BANK], F32, name="b_ps", bufs=2)
+                b_ps = psum.tile([P, BANK], F32, name="b_ps", bufs=4)
                 table_product(b_ps, w2_q, t, u)
                 half_sine = ring.tile([P, BANK], F32, name="half_sine")
                 nc.scalar.activation(half_sine[:], b_ps[:], ACT.Sin, scale=0.5)
-                nc.scalar.activation(versine[t][:, cols], half_sine[:], ACT.Square, scale=math.sqrt(2.0))
+                nc.scalar.activation(work[t][:, cols], half_sine[:], ACT.Square, scale=math.sqrt(2.0))
 
+        versine(0)
+        versine(1)
         w1_q = [
-            quantise(f"w1_{a}", round_weights(f"w1_{a}", w1_raw[a], nc.vector.tensor_copy)) for a in range(PASSES)
+            quantise(f"w1_{a}", round_weights(f"w1_{a}", w1_raw[a], nc.vector.tensor_copy), pieces=1 + a)
+            for a in range(PASSES)
         ]
 
         h = [keep.tile([P, S], F32, name=f"h{t}") for t in range(PACK)]
@@ -199,28 +231,37 @@ def tile_list_torn_strip_splice_kernel(
             )
 
         for t in range(PACK):
+            d_ps = []
+            for u in range(UNITS):
+                d_ps.append(psum.tile([P, BANK], F32, name="d_ps", bufs=2))
+                a_ps = psum.tile([P, BANK], F32, name="a_ps", bufs=2)
+                table_product_fp4(d_ps[u], t, u)
+                table_product(a_ps, w1_q, t, u)
+                row = work[t][:, u * BANK : (u + 1) * BANK]
+                nc.vector.scalar_tensor_tensor(row, row, 1.0, a_ps[:], ALU.subtract, ALU.mult)
             for u in range(UNITS):
                 cols = slice(u * BANK, (u + 1) * BANK)
-                d_ps = psum.tile([P, BANK], F32, name="d_ps", bufs=3)
-                a_ps = psum.tile([P, BANK], F32, name="a_ps", bufs=3)
-                table_product_fp4(d_ps, t, u)
-                table_product(a_ps, w1_q, t, u)
-                minus_ac = ring.tile([P, BANK], F32, name="minus_ac")
-                nc.vector.scalar_tensor_tensor(
-                    minus_ac[:], versine[t][:, cols], 1.0, a_ps[:], ALU.subtract, ALU.mult
-                )
-                larger = ring.tile([P, BANK], F32, name="larger")
-                nc.vector.scalar_tensor_tensor(larger[:], minus_ac[:], -1.0, d_ps[:], ALU.mult, ALU.max)
-                nc.scalar.activation(h[t][:, cols], larger[:], ACT.Copy, scale=gain_sb[:, t : t + 1])
-            if t > 0:
-                pick(t - 1, 0)
-            if t == 1:
-                w4_q = quantise("w4", round_weights("w4", w4_raw, nc.scalar.copy))
-        pick(PACK - 1, 0)
+                row = work[t][:, cols]
+                nc.vector.scalar_tensor_tensor(row, row, -1.0, d_ps[u][:], ALU.mult, ALU.max)
+                nc.scalar.activation(h[t][:, cols], row, ACT.Copy, scale=gain_sb[t][:])
+            if t + 2 < PACK:
+                versine(t + 2)
+        w4_bf = keep.tile([P, PACK * H], BF16, name="w4_bf", align_bytes=64)
+        for t in range(PACK):
+            nc.gpsimd.tensor_scalar(
+                w4_bf[:].rearrange("p (t b q j) -> p t b q j", t=PACK, q=RUN, j=PACK)[:, t],
+                w4_raw[:].rearrange("p j (b t q) -> p t b q j", t=PACK, q=RUN)[:, t],
+                1.0,
+                0.0,
+                ALU.mult,
+                ALU.add,
+            )
+        for t in range(PACK):
+            pick(t, 0)
 
-        def interleave(c):
+        def interleave(c, copy):
             x_bf = keep.tile([P, CHUNK * PACK], BF16, name=f"x_bf{c}", align_bytes=64)
-            nc.scalar.copy(
+            copy(
                 out=x_bf[:].rearrange("p (g i t) -> p g t i", i=4, t=PACK),
                 in_=x32[c][:].rearrange("p t (g i) -> p g t i", i=4),
             )
@@ -230,7 +271,7 @@ def tile_list_torn_strip_splice_kernel(
             ys = []
             for t in range(PACK):
                 rows = slice(t * P, (t + 1) * P)
-                y_ps = psum.tile([P, BANK], F32, name="b_ps", bufs=2)
+                y_ps = psum.tile([P, BANK], F32, name="b_ps", bufs=4)
                 nc.tensor.matmul_mx(
                     out=y_ps[:, :CHUNK],
                     lhsT=w4_q[0][:, rows].bitcast(FP8X4),
@@ -253,22 +294,25 @@ def tile_list_torn_strip_splice_kernel(
                 ALU.mult,
             )
 
-        x_bf0 = interleave(0)
-        for t in range(2):
-            pick(t, 1)
+        def keep_whole(t):
+            nc.scalar.activation(o[t][:], h[t][:], ACT.Copy, scale=skip_sb[t][:])
+
+        w4_q = quantise("w4", w4_bf)
+        x_bf0 = interleave(0, nc.vector.tensor_copy)
+        pick(0, 1)
         x_q0 = quantise("x0", x_bf0)
-        for t in range(2, PACK):
-            pick(t, 1)
-        for t in range(PACK):
-            nc.scalar.activation(o[t][:], h[t][:], ACT.Copy, scale=skip_sb[:, t : t + 1])
+        keep_whole(0)
         y0 = second_stage(0, x_q0)
-        x_bf1 = interleave(1)
+        for t in range(1, PACK):
+            pick(t, 1)
+            keep_whole(t)
         put(0, 0, y0[0])
+        x_bf1 = interleave(1, nc.vector.tensor_copy)
+        put(1, 0, y0[1])
         x_q1 = quantise("x1", x_bf1)
         y1 = second_stage(1, x_q1)
-        for t in range(1, PACK):
+        for t in range(2, PACK):
             put(t, 0, y0[t])
-        out_rows = out.rearrange("(p t) j -> p t j", t=PACK)
         for t in range(PACK):
             put(t, 1, y1[t])
-            nc.sync.dma_start(out=out_rows[:, t, :], in_=o[t][:])
+            nc.sync.dma_start(out=dealt(out)[t], in_=o[t][:])

@@ -44,12 +44,11 @@ def tile_list_torn_strip_splice_kernel(
 
         tab_s = keep.tile([P, T], U8, name="tab_s", align_bytes=64)
         v_s = keep.tile([P, S], U8, name="v_s", align_bytes=64)
-        planes = keep.tile([P, PASSES * S], U8, name="planes", align_bytes=64)
+        v_s1 = keep.tile([P, S], U8, name="v_s1", align_bytes=64)
         w3_s_raw = keep.tile([P, PASSES, H], U8, name="w3_s_raw", align_bytes=64)
-        nc.vector.memset(tab_s[32:64, :].bitcast(I32), 0)
-        nc.vector.memset(tab_s[64:128, :].bitcast(I32), 0)
-        nc.gpsimd.memset(w3_s_raw[:].rearrange("p a c -> p (a c)").bitcast(I32), 0)
-        nc.gpsimd.memset(planes[:].bitcast(I32), 0)
+        nc.vector.memset(tab_s[:].bitcast(I32), 0)
+        nc.vector.memset(w3_s_raw[:].rearrange("p a c -> p (a c)").bitcast(I32), 0)
+        nc.vector.memset(v_s1[:].bitcast(I32), 0)
 
         tab_w = [keep.tile([P, T], U32, name=f"tab_w{a}", align_bytes=64) for a in range(PASSES)]
         v_w = [keep.tile([P, S], U32, name=f"v_w{a}", align_bytes=64) for a in range(PASSES)]
@@ -90,9 +89,11 @@ def tile_list_torn_strip_splice_kernel(
             return columns
 
         nc.sync.dma_start(offs_sb[:], offs)
-        nc.sync.dma_start(
-            out=tab_s[0:32, :].bitcast(I32), in_=tab_scales.rearrange("a q t -> (a q) t").bitcast(I32)
-        )
+        for q in range(4):
+            nc.gpsimd.dma_start(
+                out=tab_s[32 * q : 32 * q + 4 * PASSES, :].bitcast(I32),
+                in_=tab_scales[:, 4 * q : 4 * q + 4, :].bitcast(I32),
+            )
         load_table_words(0)
         w2_raw = [load_rows(f"w2_{a}", w2[a * K_PASS : (a + 1) * K_PASS, :]) for a in range(PASSES)]
         load_table_words(1)
@@ -121,12 +122,11 @@ def tile_list_torn_strip_splice_kernel(
             )
 
         nc.vector.tensor_copy(v_s[:], tab_s[:].indirect(offs_sb[:]))
-        for a in range(PASSES):
-            for q in range(4):
-                nc.gpsimd.dma_start(
-                    out=planes[32 * q : 32 * q + 4, a * S : (a + 1) * S].bitcast(I32),
-                    in_=v_s[16 * a + 4 * q : 16 * a + 4 * q + 4, :].bitcast(I32),
-                )
+        for q in range(4):
+            nc.gpsimd.dma_start(
+                out=v_s1[32 * q : 32 * q + 4, :].bitcast(I32),
+                in_=v_s[32 * q + 4 : 32 * q + 8, :].bitcast(I32),
+            )
         nc.vector.tensor_copy(v_w[0][:], tab_w[0][:].indirect(offs_sb[:]))
         w3_w = keep.tile([P, PASSES * 2 * H], U8, name="w3_w", align_bytes=64)
         w3_s = keep.tile([P, PASSES * H], U8, name="w3_s", align_bytes=64)
@@ -137,7 +137,6 @@ def tile_list_torn_strip_splice_kernel(
                 in_=src[:].bitcast(I32).rearrange("p a (b t w) -> p a t b w", t=PACK, b=BLOCKS),
             )
 
-        deal_bytes(w3_s, w3_s_raw)
 
         def round_weights(name, parts, copy):
             grouped = keep.tile([P, PACK * H], BF16, name=f"{name}_bf", align_bytes=64)
@@ -169,6 +168,7 @@ def tile_list_torn_strip_splice_kernel(
                 v_w[1][:, u * BANK : (u + 1) * BANK],
                 tab_w[1][:].indirect(offs_sb[:, u * BANK // 16 : (u + 1) * BANK // 16]),
             )
+        deal_bytes(w3_s, w3_s_raw)
         deal_bytes(w3_w, w3_w_raw)
 
         def table_product(acc, weights, t, u):
@@ -181,21 +181,21 @@ def tile_list_torn_strip_splice_kernel(
                     lhsT=codes[:, rows].bitcast(FP8X4),
                     lhsT_scale=scales[:, rows],
                     rhs=v_w[a][:, cols].bitcast(FP8X4),
-                    rhs_scale=planes[:, a * S + u * BANK : a * S + (u + 1) * BANK],
+                    rhs_scale=v_s[4 * a :, cols],
                     start=(a == 0),
                     stop=(a == PASSES - 1),
                 )
 
         def table_product_fp4(acc, t, u):
             cols = slice(u * BANK, (u + 1) * BANK)
-            for a in range(PASSES):
+            for a, plane in enumerate((v_s, v_s1)):
                 c0 = a * H + t * P
                 nc.tensor.matmul_mx(
                     out=acc[:],
                     lhsT=w3_w[:, 2 * c0 : 2 * (c0 + P)].bitcast(FP4X4),
                     lhsT_scale=w3_s[:, c0 : c0 + P],
                     rhs=v_w[a][:, cols].bitcast(FP8X4),
-                    rhs_scale=planes[:, a * S + u * BANK : a * S + (u + 1) * BANK],
+                    rhs_scale=plane[:, cols],
                     start=(a == 0),
                     stop=(a == PASSES - 1),
                 )
@@ -213,10 +213,22 @@ def tile_list_torn_strip_splice_kernel(
 
         versine(0)
         versine(1)
-        w1_q = [
-            quantise(f"w1_{a}", round_weights(f"w1_{a}", w1_raw[a], nc.vector.tensor_copy), pieces=1 + a)
-            for a in range(PASSES)
-        ]
+        w1_q = [quantise("w1_0", round_weights("w1_0", w1_raw[0], nc.vector.tensor_copy))]
+        last_bf = keep.tile([P, PACK * H], BF16, name="w1_1_bf", align_bytes=64)
+        last_codes = keep.tile([P, H], U32, name="w1_1_codes", align_bytes=64)
+        last_scales = keep.tile([P, H], U8, name="w1_1_scales", align_bytes=64)
+        dst = last_bf[:].rearrange("p (t b q j) -> p t b q j", t=PACK, q=RUN, j=PACK)
+        src = [raw[:].rearrange("p j (b t q) -> p t b q j", t=PACK, q=RUN) for raw in w1_raw[1]]
+        nc.vector.tensor_copy(out=dst[:, :, : BLOCKS // 2], in_=src[0])
+        for t0 in range(0, PACK, 2):
+            nc.vector.tensor_copy(out=dst[:, t0 : t0 + 2, BLOCKS // 2 :], in_=src[1][:, t0 : t0 + 2])
+            cols = slice(t0 * P, (t0 + 2) * P)
+            nc.vector.quantize_mx(
+                out=last_codes[:, cols].bitcast(FP8X4),
+                scales=last_scales[:, cols],
+                in_=last_bf[:, PACK * t0 * P : PACK * (t0 + 2) * P],
+            )
+        w1_q.append((last_codes, last_scales))
 
         h = [keep.tile([P, S], F32, name=f"h{t}") for t in range(PACK)]
         o = [keep.tile([P, S], F32, name=f"o{t}") for t in range(PACK)]

@@ -28,6 +28,19 @@ BLOCKS = H // 32
 CHUNK = 256
 CHUNKS = M // CHUNK
 
+B_BANKS = ((0, 1), (2, 3), (0, 1), (2, 4))
+A_BANKS = ((4, 5), (3, 5), (3, 5), (3, 5))
+D_BANKS = (6, 7)
+
+AT_W2_1 = 0
+AT_TAB_S = 8192 - 64
+AT_W3_W = 8192
+AT_W3_S = AT_W3_W + 2048
+AT_FACTORS = AT_W3_S + 1024
+AT_TAB_W1 = AT_TAB_S + 4096 - 64
+AT_TAB_W0 = AT_TAB_W1 + 16384
+AT_W2_0 = AT_TAB_W0 + 16384
+
 
 def tile_list_torn_strip_splice_kernel(
     tc, tab_words, tab_scales, offs, pos1, w1, w2, w3_words, w3_scales, gain, splice, w4, skip, wgo, out
@@ -36,98 +49,94 @@ def tile_list_torn_strip_splice_kernel(
     with ExitStack() as ctx:
         lists = ctx.enter_context(tc.tile_pool(name="lists", bufs=1))
         keep = ctx.enter_context(tc.tile_pool(name="keep", bufs=1))
+        stage = ctx.enter_context(tc.tile_pool(name="stage", bufs=1))
+        late = ctx.enter_context(tc.tile_pool(name="late", bufs=1))
         ring = ctx.enter_context(tc.tile_pool(name="ring", bufs=3))
         psum = ctx.enter_context(tc.psum_pool(name="psum", bufs=1))
 
         offs_sb = lists.tile([P, S // 16], U16, name="offs_sb")
         pos_sb = lists.tile([P, M // 16], U16, name="pos_sb")
 
-        tab_s = keep.tile([P, T], U8, name="tab_s", align_bytes=64)
         v_s = keep.tile([P, S], U8, name="v_s", align_bytes=64)
-        v_s1 = keep.tile([P, S], U8, name="v_s1", align_bytes=64)
-        w3_s_raw = keep.tile([P, PASSES, H], U8, name="w3_s_raw", align_bytes=64)
-        nc.vector.memset(tab_s[:].bitcast(I32), 0)
-        nc.vector.memset(w3_s_raw[:].rearrange("p a c -> p (a c)").bitcast(I32), 0)
-        nc.vector.memset(v_s1[:].bitcast(I32), 0)
-
-        tab_w = [keep.tile([P, T], U32, name=f"tab_w{a}", align_bytes=64) for a in range(PASSES)]
+        planes = keep.tile([P, PASSES * S], U8, name="planes", align_bytes=64)
         v_w = [keep.tile([P, S], U32, name=f"v_w{a}", align_bytes=64) for a in range(PASSES)]
 
-        def load_table_words(a):
-            nc.sync.dma_start(
-                out=tab_w[a][:].bitcast(I32),
-                in_=tab_words[a].rearrange("p t i -> p (t i)").bitcast(I32),
-            )
+        def staged(name, shape, dtype, offset):
+            return stage.tile(shape, dtype, name=name, align_bytes=64, offset=offset)
 
-        def load_rows(name, rows, pieces=1):
-            width = H // pieces
-            parts = []
-            for i in range(pieces):
-                raw = keep.tile([P, PACK, width], F32, name=f"{name}_raw{i}")
-                nc.sync.dma_start(
-                    out=raw[:],
-                    in_=rows[:, i * width : (i + 1) * width].rearrange("(p j) c -> p j c", j=PACK),
-                )
-                parts.append(raw)
-            return parts
+        def load_table_words(a, offset):
+            words = staged(f"tab_w{a}", [P, T], U32, offset)
+            nc.sync.dma_start(
+                out=words[:].bitcast(I32), in_=tab_words[a].rearrange("p t i -> p (t i)").bitcast(I32)
+            )
+            return words
+
+        def load_rows(name, rows, offset):
+            raw = staged(name, [P, PACK, rows.shape[1]], F32, offset)
+            nc.sync.dma_start(out=raw[:], in_=rows.rearrange("(p j) c -> p j c", j=PACK))
+            return raw
 
         def dealt(rows):
             return rows.rearrange("(b t q) c -> t b q c", t=PACK, q=RUN)
 
-        def load_dealt(name, rows):
-            slots = keep.tile([P, PACK, rows.shape[1]], F32, name=name)
+        def load_dealt(name, rows, offset):
+            slots = staged(name, [P, PACK, rows.shape[1]], F32, offset)
             for t in range(PACK):
                 nc.sync.dma_start(out=slots[:, t, :], in_=dealt(rows)[t])
             return slots
 
-        def load_factors(name, vec):
+        def load_factors(name, vec, offset):
             columns = []
             for t in range(PACK):
-                column = keep.tile([P, 1], F32, name=f"{name}{t}")
+                column = staged(f"{name}{t}", [P, 1], F32, offset + 64 * t)
                 nc.sync.dma_start(out=column[:], in_=dealt(vec.unsqueeze(1))[t], allow_slow_non_contiguous=True)
                 columns.append(column)
             return columns
 
+        def move_scale_rows(first, last):
+            for a, q in [divmod(i, 4) for i in range(first, last)]:
+                nc.sync.dma_start(
+                    out=planes[32 * q : 32 * q + 4, a * S : (a + 1) * S].bitcast(I32),
+                    in_=v_s[16 * a + 4 * q : 16 * a + 4 * q + 4, :].bitcast(I32),
+                )
+
+        tab_s = staged("tab_s", [P, T], U8, AT_TAB_S)
+        nc.vector.memset(tab_s[32:64, :].bitcast(I32), 0)
+        nc.vector.memset(tab_s[64:128, :].bitcast(I32), 0)
+        nc.gpsimd.memset(planes[:].bitcast(I32), 0)
         nc.sync.dma_start(offs_sb[:], offs)
-        for q in range(4):
-            nc.gpsimd.dma_start(
-                out=tab_s[32 * q : 32 * q + 4 * PASSES, :].bitcast(I32),
-                in_=tab_scales[:, 4 * q : 4 * q + 4, :].bitcast(I32),
-            )
-        load_table_words(0)
-        w2_raw = [load_rows(f"w2_{a}", w2[a * K_PASS : (a + 1) * K_PASS, :]) for a in range(PASSES)]
-        load_table_words(1)
-        w3_w_raw = keep.tile([P, PASSES, 2 * H], U8, name="w3_w_raw", align_bytes=64)
+        nc.sync.dma_start(
+            out=tab_s[0:32, :].bitcast(I32), in_=tab_scales.rearrange("a q t -> (a q) t").bitcast(I32)
+        )
+        tab_w = [load_table_words(0, AT_TAB_W0)]
+        w2_raw = [[load_rows("w2_0_raw", w2[:K_PASS, :], AT_W2_0)]]
+        nc.sync.dma_start(pos_sb[:], pos1)
+        nc.vector.tensor_copy(v_s[:], tab_s[:].indirect(offs_sb[:]))
+        nc.vector.tensor_copy(v_w[0][:], tab_w[0][:].indirect(offs_sb[:]))
+
+        move_scale_rows(0, 5)
+        tab_w.append(load_table_words(1, AT_TAB_W1))
+        move_scale_rows(5, 8)
+        w2_raw.append([load_rows("w2_1_raw", w2[K_PASS:, :], AT_W2_1)])
+        w3_w_raw = staged("w3_w_raw", [P, PASSES, 2 * H], U8, AT_W3_W)
         nc.sync.dma_start(
             out=w3_w_raw[:].bitcast(I32), in_=w3_words.rearrange("a p c -> p a c").bitcast(I32)
         )
-        w1_raw = [
-            load_rows(f"w1_{a}", w1[a * K_PASS : (a + 1) * K_PASS, :], pieces=1 + a) for a in range(PASSES)
-        ]
-        w4_raw = load_dealt("w4_raw", w4)
-        gain_sb = load_factors("gain", gain)
-        nc.sync.dma_start(pos_sb[:], pos1)
-        splice_sb = load_dealt("splice_sb", splice)
-        skip_sb = load_factors("skip", skip)
-        wgo_sb = keep.tile([P, PACK * M], F32, name="wgo_sb")
-        for t in range(PACK):
-            nc.sync.dma_start(out=wgo_sb[0:32, t * M : (t + 1) * M], in_=dealt(wgo)[t])
-        for q in range(1, 4):
-            nc.sync.dma_start(out=wgo_sb[32 * q : 32 * q + 32, :], in_=wgo_sb[0:32, :])
-
+        w3_s_raw = staged("w3_s_raw", [P, PASSES, H], U8, AT_W3_S)
+        nc.vector.memset(w3_s_raw[:].rearrange("p a c -> p (a c)").bitcast(I32), 0)
         for q in range(4):
-            nc.gpsimd.dma_start(
+            nc.sync.dma_start(
                 out=w3_s_raw[32 * q : 32 * q + 4, :, :].bitcast(I32),
                 in_=w3_scales[:, 4 * q : 4 * q + 4, :].rearrange("a r c -> r a c").bitcast(I32),
             )
+        w1_raw = [
+            [load_rows("w1_0_raw", w1[:K_PASS, :], AT_TAB_W0)],
+            [
+                load_rows(f"w1_1_raw{i}", w1[K_PASS:, i * H // 2 : (i + 1) * H // 2], AT_TAB_W0 + 8192 + 4096 * i)
+                for i in range(2)
+            ],
+        ]
 
-        nc.vector.tensor_copy(v_s[:], tab_s[:].indirect(offs_sb[:]))
-        for q in range(4):
-            nc.gpsimd.dma_start(
-                out=v_s1[32 * q : 32 * q + 4, :].bitcast(I32),
-                in_=v_s[32 * q + 4 : 32 * q + 8, :].bitcast(I32),
-            )
-        nc.vector.tensor_copy(v_w[0][:], tab_w[0][:].indirect(offs_sb[:]))
         w3_w = keep.tile([P, PASSES * 2 * H], U8, name="w3_w", align_bytes=64)
         w3_s = keep.tile([P, PASSES * H], U8, name="w3_s", align_bytes=64)
 
@@ -149,9 +158,10 @@ def tile_list_torn_strip_splice_kernel(
                 )
             return grouped
 
-        def quantise(name, grouped, pieces=1):
+        def quantise(name, grouped, pieces=1, codes=None):
             width = grouped.shape[1] // PACK
-            codes = keep.tile([P, width], U32, name=f"{name}_codes", align_bytes=64)
+            if codes is None:
+                codes = keep.tile([P, width], U32, name=f"{name}_codes", align_bytes=64)
             scales = keep.tile([P, width], U8, name=f"{name}_scales", align_bytes=64)
             step = width // pieces
             for c0 in range(0, width, step):
@@ -162,57 +172,80 @@ def tile_list_torn_strip_splice_kernel(
                 )
             return codes, scales
 
-        w2_q = [quantise(f"w2_{a}", round_weights(f"w2_{a}", w2_raw[a], nc.vector.tensor_copy)) for a in range(PASSES)]
-        for u in range(UNITS):
-            nc.vector.tensor_copy(
-                v_w[1][:, u * BANK : (u + 1) * BANK],
-                tab_w[1][:].indirect(offs_sb[:, u * BANK // 16 : (u + 1) * BANK // 16]),
-            )
-        deal_bytes(w3_s, w3_s_raw)
+        w2_q = [quantise("w2_0", round_weights("w2_0", w2_raw[0], nc.vector.tensor_copy))]
+        nc.vector.tensor_copy(v_w[1][:], tab_w[1][:].indirect(offs_sb[:]))
+        w2_q.append(quantise("w2_1", round_weights("w2_1", w2_raw[1], nc.vector.tensor_copy), pieces=2))
         deal_bytes(w3_w, w3_w_raw)
+        deal_bytes(w3_s, w3_s_raw)
 
-        def table_product(acc, weights, t, u):
+        w4_raw = load_dealt("w4_raw", w4, AT_W2_0)
+        gain_sb = load_factors("gain", gain, AT_FACTORS)
+        splice_sb = load_dealt("splice_sb", splice, AT_W2_1)
+        skip_sb = load_factors("skip", skip, AT_FACTORS + 256)
+        wgo_sb = staged("wgo_sb", [P, PACK * M], F32, AT_TAB_W1)
+        for t in range(PACK):
+            nc.sync.dma_start(out=wgo_sb[0:32, t * M : (t + 1) * M], in_=dealt(wgo)[t])
+        for q in range(1, 4):
+            nc.sync.dma_start(out=wgo_sb[32 * q : 32 * q + 32, :], in_=wgo_sb[0:32, :])
+
+        def bank(index):
+            return psum.tile([P, BANK], F32, name=f"bank{index}")
+
+        def table_product(acc, weights, t, u, order):
             cols = slice(u * BANK, (u + 1) * BANK)
             rows = slice(t * P, (t + 1) * P)
-            for a in range(PASSES):
+            for a in order:
                 codes, scales = weights[a]
                 nc.tensor.matmul_mx(
                     out=acc[:],
                     lhsT=codes[:, rows].bitcast(FP8X4),
                     lhsT_scale=scales[:, rows],
                     rhs=v_w[a][:, cols].bitcast(FP8X4),
-                    rhs_scale=v_s[4 * a :, cols],
-                    start=(a == 0),
-                    stop=(a == PASSES - 1),
+                    rhs_scale=planes[:, a * S + u * BANK : a * S + (u + 1) * BANK],
+                    start=(a == order[0]),
+                    stop=(a == order[-1]),
                 )
 
         def table_product_fp4(acc, t, u):
             cols = slice(u * BANK, (u + 1) * BANK)
-            for a, plane in enumerate((v_s, v_s1)):
+            for a in range(PASSES):
                 c0 = a * H + t * P
                 nc.tensor.matmul_mx(
                     out=acc[:],
                     lhsT=w3_w[:, 2 * c0 : 2 * (c0 + P)].bitcast(FP4X4),
                     lhsT_scale=w3_s[:, c0 : c0 + P],
                     rhs=v_w[a][:, cols].bitcast(FP8X4),
-                    rhs_scale=plane[:, cols],
+                    rhs_scale=planes[:, a * S + u * BANK : a * S + (u + 1) * BANK],
                     start=(a == 0),
                     stop=(a == PASSES - 1),
                 )
 
-        work = [keep.tile([P, S], F32, name=f"work{t}") for t in range(PACK)]
+        work = [keep.tile([P, S], F32, name=f"work{t}") for t in range(PACK - 1)]
+        work.append(late.tile([P, S], F32, name="work_last", align_bytes=64, offset=2048))
 
-        def versine(t):
-            for u in range(UNITS):
-                cols = slice(u * BANK, (u + 1) * BANK)
-                b_ps = psum.tile([P, BANK], F32, name="b_ps", bufs=4)
-                table_product(b_ps, w2_q, t, u)
-                half_sine = ring.tile([P, BANK], F32, name="half_sine")
-                nc.scalar.activation(half_sine[:], b_ps[:], ACT.Sin, scale=0.5)
-                nc.scalar.activation(work[t][:, cols], half_sine[:], ACT.Square, scale=math.sqrt(2.0))
+        half_sines = {}
 
-        versine(0)
-        versine(1)
+        def sine(step):
+            t, u = divmod(step, UNITS)
+            b_ps = bank(B_BANKS[t][u])
+            table_product(b_ps, w2_q, t, u, (0, 1))
+            half_sines[step] = ring.tile([P, BANK], F32, name="half_sine")
+            nc.scalar.activation(half_sines[step][:], b_ps[:], ACT.Sin, scale=0.5)
+
+        def square(step):
+            t, u = divmod(step, UNITS)
+            nc.scalar.activation(
+                work[t][:, u * BANK : (u + 1) * BANK], half_sines[step][:], ACT.Square, scale=math.sqrt(2.0)
+            )
+
+        def versine_steps(first, last):
+            for step in range(first, last):
+                if step < PACK * UNITS:
+                    sine(step)
+                if 0 < step <= PACK * UNITS:
+                    square(step - 1)
+
+        versine_steps(0, 2 * UNITS)
         w1_q = [quantise("w1_0", round_weights("w1_0", w1_raw[0], nc.vector.tensor_copy))]
         last_bf = keep.tile([P, PACK * H], BF16, name="w1_1_bf", align_bytes=64)
         last_codes = keep.tile([P, H], U32, name="w1_1_codes", align_bytes=64)
@@ -220,18 +253,18 @@ def tile_list_torn_strip_splice_kernel(
         dst = last_bf[:].rearrange("p (t b q j) -> p t b q j", t=PACK, q=RUN, j=PACK)
         src = [raw[:].rearrange("p j (b t q) -> p t b q j", t=PACK, q=RUN) for raw in w1_raw[1]]
         nc.vector.tensor_copy(out=dst[:, :, : BLOCKS // 2], in_=src[0])
-        for t0 in range(0, PACK, 2):
-            nc.vector.tensor_copy(out=dst[:, t0 : t0 + 2, BLOCKS // 2 :], in_=src[1][:, t0 : t0 + 2])
-            cols = slice(t0 * P, (t0 + 2) * P)
+        for t0, t1 in ((0, 1), (1, 2), (2, 4)):
+            nc.vector.tensor_copy(out=dst[:, t0:t1, BLOCKS // 2 :], in_=src[1][:, t0:t1])
+            cols = slice(t0 * P, t1 * P)
             nc.vector.quantize_mx(
                 out=last_codes[:, cols].bitcast(FP8X4),
                 scales=last_scales[:, cols],
-                in_=last_bf[:, PACK * t0 * P : PACK * (t0 + 2) * P],
+                in_=last_bf[:, PACK * t0 * P : PACK * t1 * P],
             )
         w1_q.append((last_codes, last_scales))
 
         h = [keep.tile([P, S], F32, name=f"h{t}") for t in range(PACK)]
-        o = [keep.tile([P, S], F32, name=f"o{t}") for t in range(PACK)]
+        o = []
         x32 = [keep.tile([P, PACK, CHUNK], F32, name=f"x32_{c}") for c in range(CHUNKS)]
 
         def pick(t, c):
@@ -245,10 +278,10 @@ def tile_list_torn_strip_splice_kernel(
         for t in range(PACK):
             d_ps = []
             for u in range(UNITS):
-                d_ps.append(psum.tile([P, BANK], F32, name="d_ps", bufs=2))
-                a_ps = psum.tile([P, BANK], F32, name="a_ps", bufs=2)
+                d_ps.append(bank(D_BANKS[u]))
+                a_ps = bank(A_BANKS[t][u])
                 table_product_fp4(d_ps[u], t, u)
-                table_product(a_ps, w1_q, t, u)
+                table_product(a_ps, w1_q, t, u, (0, 1) if t == 0 else (1, 0))
                 row = work[t][:, u * BANK : (u + 1) * BANK]
                 nc.vector.scalar_tensor_tensor(row, row, 1.0, a_ps[:], ALU.subtract, ALU.mult)
             for u in range(UNITS):
@@ -256,8 +289,7 @@ def tile_list_torn_strip_splice_kernel(
                 row = work[t][:, cols]
                 nc.vector.scalar_tensor_tensor(row, row, -1.0, d_ps[u][:], ALU.mult, ALU.max)
                 nc.scalar.activation(h[t][:, cols], row, ACT.Copy, scale=gain_sb[t][:])
-            if t + 2 < PACK:
-                versine(t + 2)
+            versine_steps((t + 2) * UNITS, (t + 3) * UNITS)
         w4_bf = keep.tile([P, PACK * H], BF16, name="w4_bf", align_bytes=64)
         for t in range(PACK):
             nc.gpsimd.tensor_scalar(
@@ -283,7 +315,7 @@ def tile_list_torn_strip_splice_kernel(
             ys = []
             for t in range(PACK):
                 rows = slice(t * P, (t + 1) * P)
-                y_ps = psum.tile([P, BANK], F32, name="b_ps", bufs=4)
+                y_ps = bank(PACK * c + t)
                 nc.tensor.matmul_mx(
                     out=y_ps[:, :CHUNK],
                     lhsT=w4_q[0][:, rows].bitcast(FP8X4),
@@ -307,12 +339,13 @@ def tile_list_torn_strip_splice_kernel(
             )
 
         def keep_whole(t):
+            o.append(late.tile([P, S], F32, name=f"o{t}", align_bytes=64, offset=4096 * t))
             nc.scalar.activation(o[t][:], h[t][:], ACT.Copy, scale=skip_sb[t][:])
 
         w4_q = quantise("w4", w4_bf)
         x_bf0 = interleave(0, nc.vector.tensor_copy)
         pick(0, 1)
-        x_q0 = quantise("x0", x_bf0)
+        x_q0 = quantise("x0", x_bf0, codes=late.tile([P, CHUNK], U32, name="x0_codes", align_bytes=64, offset=11776))
         keep_whole(0)
         y0 = second_stage(0, x_q0)
         for t in range(1, PACK):

import math
from contextlib import ExitStack

import concourse.mybir as mybir

K, T, S, M, H = 1024, 4096, 1024, 512, 512
FLOPS = 2 * (3 * K * H * S + H * H * M)

F32 = mybir.dt.float32
BF16 = mybir.dt.bfloat16
I32 = mybir.dt.int32
U32 = mybir.dt.uint32
U16 = mybir.dt.uint16
U8 = mybir.dt.uint8
FP8X4 = mybir.dt.float8_e4m3fn_x4
FP4X4 = mybir.dt.float4_e2m1fn_x4
ACT = mybir.ActivationFunctionType
ALU = mybir.AluOpType

P = 128
PACK = 4
K_PASS = P * PACK
PASSES = K // K_PASS
BANK = 512
UNITS = S // BANK
RUN = 8
BLOCKS = H // 32
CHUNK = 256
CHUNKS = M // CHUNK

B_BANKS = ((0, 1), (2, 3), (0, 1), (2, 4))
A_BANKS = ((4, 5), (3, 5), (3, 5), (3, 5))
D_BANKS = (6, 7)

AT_W2_1 = 0
AT_TAB_S = 8192 - 64
AT_W3_W = 8192
AT_W3_S = AT_W3_W + 2048
AT_FACTORS = AT_W3_S + 1024
AT_TAB_W1 = AT_TAB_S + 4096 - 64
AT_TAB_W0 = AT_TAB_W1 + 16384
AT_W2_0 = AT_TAB_W0 + 16384


def tile_list_torn_strip_splice_kernel(
    tc, tab_words, tab_scales, offs, pos1, w1, w2, w3_words, w3_scales, gain, splice, w4, skip, wgo, out
):
    nc = tc.nc
    with ExitStack() as ctx:
        lists = ctx.enter_context(tc.tile_pool(name="lists", bufs=1))
        keep = ctx.enter_context(tc.tile_pool(name="keep", bufs=1))
        stage = ctx.enter_context(tc.tile_pool(name="stage", bufs=1))
        late = ctx.enter_context(tc.tile_pool(name="late", bufs=1))
        ring = ctx.enter_context(tc.tile_pool(name="ring", bufs=3))
        psum = ctx.enter_context(tc.psum_pool(name="psum", bufs=1))

        offs_sb = lists.tile([P, S // 16], U16, name="offs_sb")
        pos_sb = lists.tile([P, M // 16], U16, name="pos_sb")

        v_s = keep.tile([P, S], U8, name="v_s", align_bytes=64)
        planes = keep.tile([P, PASSES * S], U8, name="planes", align_bytes=64)
        v_w = [keep.tile([P, S], U32, name=f"v_w{a}", align_bytes=64) for a in range(PASSES)]

        def staged(name, shape, dtype, offset):
            return stage.tile(shape, dtype, name=name, align_bytes=64, offset=offset)

        def load_table_words(a, offset):
            words = staged(f"tab_w{a}", [P, T], U32, offset)
            nc.sync.dma_start(
                out=words[:].bitcast(I32), in_=tab_words[a].rearrange("p t i -> p (t i)").bitcast(I32)
            )
            return words

        def load_rows(name, rows, offset):
            raw = staged(name, [P, PACK, rows.shape[1]], F32, offset)
            nc.sync.dma_start(out=raw[:], in_=rows.rearrange("(p j) c -> p j c", j=PACK))
            return raw

        def dealt(rows):
            return rows.rearrange("(b t q) c -> t b q c", t=PACK, q=RUN)

        def load_dealt(name, rows, offset):
            slots = staged(name, [P, PACK, rows.shape[1]], F32, offset)
            for t in range(PACK):
                nc.sync.dma_start(out=slots[:, t, :], in_=dealt(rows)[t])
            return slots

        def load_factors(name, vec, offset):
            columns = []
            for t in range(PACK):
                column = staged(f"{name}{t}", [P, 1], F32, offset + 64 * t)
                nc.sync.dma_start(out=column[:], in_=dealt(vec.unsqueeze(1))[t], allow_slow_non_contiguous=True)
                columns.append(column)
            return columns

        def move_scale_rows(first, last):
            for a, q in [divmod(i, 4) for i in range(first, last)]:
                nc.sync.dma_start(
                    out=planes[32 * q : 32 * q + 4, a * S : (a + 1) * S].bitcast(I32),
                    in_=v_s[16 * a + 4 * q : 16 * a + 4 * q + 4, :].bitcast(I32),
                )

        tab_s = staged("tab_s", [P, T], U8, AT_TAB_S)
        nc.vector.memset(tab_s[32:64, :].bitcast(I32), 0)
        nc.vector.memset(tab_s[64:128, :].bitcast(I32), 0)
        nc.gpsimd.memset(planes[:].bitcast(I32), 0)
        nc.sync.dma_start(offs_sb[:], offs)
        nc.sync.dma_start(
            out=tab_s[0:32, :].bitcast(I32), in_=tab_scales.rearrange("a q t -> (a q) t").bitcast(I32)
        )
        tab_w = [load_table_words(0, AT_TAB_W0)]
        w2_raw = [[load_rows("w2_0_raw", w2[:K_PASS, :], AT_W2_0)]]
        nc.sync.dma_start(pos_sb[:], pos1)
        nc.vector.tensor_copy(v_s[:], tab_s[:].indirect(offs_sb[:]))
        nc.vector.tensor_copy(v_w[0][:], tab_w[0][:].indirect(offs_sb[:]))

        move_scale_rows(0, 5)
        tab_w.append(load_table_words(1, AT_TAB_W1))
        move_scale_rows(5, 8)
        w2_raw.append([load_rows("w2_1_raw", w2[K_PASS:, :], AT_W2_1)])
        w3_w_raw = staged("w3_w_raw", [P, PASSES, 2 * H], U8, AT_W3_W)
        nc.sync.dma_start(
            out=w3_w_raw[:].bitcast(I32), in_=w3_words.rearrange("a p c -> p a c").bitcast(I32)
        )
        w3_s_raw = staged("w3_s_raw", [P, PASSES, H], U8, AT_W3_S)
        nc.vector.memset(w3_s_raw[:].rearrange("p a c -> p (a c)").bitcast(I32), 0)
        for q in range(4):
            nc.sync.dma_start(
                out=w3_s_raw[32 * q : 32 * q + 4, :, :].bitcast(I32),
                in_=w3_scales[:, 4 * q : 4 * q + 4, :].rearrange("a r c -> r a c").bitcast(I32),
            )
        w1_raw = [
            [load_rows("w1_0_raw", w1[:K_PASS, :], AT_TAB_W0)],
            [
                load_rows(f"w1_1_raw{i}", w1[K_PASS:, i * H // 2 : (i + 1) * H // 2], AT_TAB_W0 + 8192 + 4096 * i)
                for i in range(2)
            ],
        ]

        w3_w = keep.tile([P, PASSES * 2 * H], U8, name="w3_w", align_bytes=64)
        w3_s = keep.tile([P, PASSES * H], U8, name="w3_s", align_bytes=64)

        def deal_bytes(dst, src):
            nc.vector.tensor_copy(
                out=dst[:].bitcast(I32).rearrange("p (a t b w) -> p a t b w", a=PASSES, t=PACK, b=BLOCKS),
                in_=src[:].bitcast(I32).rearrange("p a (b t w) -> p a t b w", t=PACK, b=BLOCKS),
            )


        def round_weights(name, parts, copy):
            grouped = keep.tile([P, PACK * H], BF16, name=f"{name}_bf", align_bytes=64)
            dst = grouped[:].rearrange("p (t b q j) -> p t b q j", t=PACK, q=RUN, j=PACK)
            bs = BLOCKS // len(parts)
            for i, raw in enumerate(parts):
                copy(
                    out=dst[:, :, i * bs : (i + 1) * bs],
                    in_=raw[:].rearrange("p j (b t q) -> p t b q j", t=PACK, q=RUN),
                )
            return grouped

        def quantise(name, grouped, pieces=1, codes=None):
            width = grouped.shape[1] // PACK
            if codes is None:
                codes = keep.tile([P, width], U32, name=f"{name}_codes", align_bytes=64)
            scales = keep.tile([P, width], U8, name=f"{name}_scales", align_bytes=64)
            step = width // pieces
            for c0 in range(0, width, step):
                nc.vector.quantize_mx(
                    out=codes[:, c0 : c0 + step].bitcast(FP8X4),
                    scales=scales[:, c0 : c0 + step],
                    in_=grouped[:, PACK * c0 : PACK * (c0 + step)],
                )
            return codes, scales

        w2_q = [quantise("w2_0", round_weights("w2_0", w2_raw[0], nc.vector.tensor_copy))]
        nc.vector.tensor_copy(v_w[1][:], tab_w[1][:].indirect(offs_sb[:]))
        w2_q.append(quantise("w2_1", round_weights("w2_1", w2_raw[1], nc.vector.tensor_copy), pieces=2))
        deal_bytes(w3_w, w3_w_raw)
        deal_bytes(w3_s, w3_s_raw)

        w4_raw = load_dealt("w4_raw", w4, AT_W2_0)
        gain_sb = load_factors("gain", gain, AT_FACTORS)
        splice_sb = load_dealt("splice_sb", splice, AT_W2_1)
        skip_sb = load_factors("skip", skip, AT_FACTORS + 256)
        wgo_sb = staged("wgo_sb", [P, PACK * M], F32, AT_TAB_W1)
        for t in range(PACK):
            nc.sync.dma_start(out=wgo_sb[0:32, t * M : (t + 1) * M], in_=dealt(wgo)[t])
        for q in range(1, 4):
            nc.sync.dma_start(out=wgo_sb[32 * q : 32 * q + 32, :], in_=wgo_sb[0:32, :])

        def bank(index):
            return psum.tile([P, BANK], F32, name=f"bank{index}")

        def table_product(acc, weights, t, u, order):
            cols = slice(u * BANK, (u + 1) * BANK)
            rows = slice(t * P, (t + 1) * P)
            for a in order:
                codes, scales = weights[a]
                nc.tensor.matmul_mx(
                    out=acc[:],
                    lhsT=codes[:, rows].bitcast(FP8X4),
                    lhsT_scale=scales[:, rows],
                    rhs=v_w[a][:, cols].bitcast(FP8X4),
                    rhs_scale=planes[:, a * S + u * BANK : a * S + (u + 1) * BANK],
                    start=(a == order[0]),
                    stop=(a == order[-1]),
                )

        def table_product_fp4(acc, t, u):
            cols = slice(u * BANK, (u + 1) * BANK)
            for a in range(PASSES):
                c0 = a * H + t * P
                nc.tensor.matmul_mx(
                    out=acc[:],
                    lhsT=w3_w[:, 2 * c0 : 2 * (c0 + P)].bitcast(FP4X4),
                    lhsT_scale=w3_s[:, c0 : c0 + P],
                    rhs=v_w[a][:, cols].bitcast(FP8X4),
                    rhs_scale=planes[:, a * S + u * BANK : a * S + (u + 1) * BANK],
                    start=(a == 0),
                    stop=(a == PASSES - 1),
                )

        work = [keep.tile([P, S], F32, name=f"work{t}") for t in range(PACK - 1)]
        work.append(late.tile([P, S], F32, name="work_last", align_bytes=64, offset=2048))

        half_sines = {}

        def sine(step):
            t, u = divmod(step, UNITS)
            b_ps = bank(B_BANKS[t][u])
            table_product(b_ps, w2_q, t, u, (0, 1))
            half_sines[step] = ring.tile([P, BANK], F32, name="half_sine")
            nc.scalar.activation(half_sines[step][:], b_ps[:], ACT.Sin, scale=0.5)

        def square(step):
            t, u = divmod(step, UNITS)
            nc.scalar.activation(
                work[t][:, u * BANK : (u + 1) * BANK], half_sines[step][:], ACT.Square, scale=math.sqrt(2.0)
            )

        def versine_steps(first, last):
            for step in range(first, last):
                if step < PACK * UNITS:
                    sine(step)
                if 0 < step <= PACK * UNITS:
                    square(step - 1)

        versine_steps(0, 2 * UNITS)
        w1_q = [quantise("w1_0", round_weights("w1_0", w1_raw[0], nc.vector.tensor_copy))]
        last_bf = keep.tile([P, PACK * H], BF16, name="w1_1_bf", align_bytes=64)
        last_codes = keep.tile([P, H], U32, name="w1_1_codes", align_bytes=64)
        last_scales = keep.tile([P, H], U8, name="w1_1_scales", align_bytes=64)
        dst = last_bf[:].rearrange("p (t b q j) -> p t b q j", t=PACK, q=RUN, j=PACK)
        src = [raw[:].rearrange("p j (b t q) -> p t b q j", t=PACK, q=RUN) for raw in w1_raw[1]]
        nc.vector.tensor_copy(out=dst[:, :, : BLOCKS // 2], in_=src[0])
        for t0, t1 in ((0, 1), (1, 2), (2, 4)):
            nc.vector.tensor_copy(out=dst[:, t0:t1, BLOCKS // 2 :], in_=src[1][:, t0:t1])
            cols = slice(t0 * P, t1 * P)
            nc.vector.quantize_mx(
                out=last_codes[:, cols].bitcast(FP8X4),
                scales=last_scales[:, cols],
                in_=last_bf[:, PACK * t0 * P : PACK * t1 * P],
            )
        w1_q.append((last_codes, last_scales))

        h = [keep.tile([P, S], F32, name=f"h{t}") for t in range(PACK)]
        o = []
        x32 = [keep.tile([P, PACK, CHUNK], F32, name=f"x32_{c}") for c in range(CHUNKS)]

        def pick(t, c):
            nc.vector.tensor_tensor(
                x32[c][:, t, :],
                h[t][:].indirect(pos_sb[:, c * CHUNK // 16 : (c + 1) * CHUNK // 16]),
                splice_sb[:, t, c * CHUNK : (c + 1) * CHUNK],
                ALU.add,
            )

        for t in range(PACK):
            d_ps = []
            for u in range(UNITS):
                d_ps.append(bank(D_BANKS[u]))
                a_ps = bank(A_BANKS[t][u])
                table_product_fp4(d_ps[u], t, u)
                table_product(a_ps, w1_q, t, u, (0, 1) if t == 0 else (1, 0))
                row = work[t][:, u * BANK : (u + 1) * BANK]
                nc.vector.scalar_tensor_tensor(row, row, 1.0, a_ps[:], ALU.subtract, ALU.mult)
            for u in range(UNITS):
                cols = slice(u * BANK, (u + 1) * BANK)
                row = work[t][:, cols]
                nc.vector.scalar_tensor_tensor(row, row, -1.0, d_ps[u][:], ALU.mult, ALU.max)
                nc.scalar.activation(h[t][:, cols], row, ACT.Copy, scale=gain_sb[t][:])
            versine_steps((t + 2) * UNITS, (t + 3) * UNITS)
        w4_bf = keep.tile([P, PACK * H], BF16, name="w4_bf", align_bytes=64)
        for t in range(PACK):
            nc.gpsimd.tensor_scalar(
                w4_bf[:].rearrange("p (t b q j) -> p t b q j", t=PACK, q=RUN, j=PACK)[:, t],
                w4_raw[:].rearrange("p j (b t q) -> p t b q j", t=PACK, q=RUN)[:, t],
                1.0,
                0.0,
                ALU.mult,
                ALU.add,
            )
        for t in range(PACK):
            pick(t, 0)

        def interleave(c, copy):
            x_bf = keep.tile([P, CHUNK * PACK], BF16, name=f"x_bf{c}", align_bytes=64)
            copy(
                out=x_bf[:].rearrange("p (g i t) -> p g t i", i=4, t=PACK),
                in_=x32[c][:].rearrange("p t (g i) -> p g t i", i=4),
            )
            return x_bf

        def second_stage(c, x_q):
            ys = []
            for t in range(PACK):
                rows = slice(t * P, (t + 1) * P)
                y_ps = bank(PACK * c + t)
                nc.tensor.matmul_mx(
                    out=y_ps[:, :CHUNK],
                    lhsT=w4_q[0][:, rows].bitcast(FP8X4),
                    lhsT_scale=w4_q[1][:, rows],
                    rhs=x_q[0][:].bitcast(FP8X4),
                    rhs_scale=x_q[1][:],
                    start=True,
                    stop=True,
                )
                y = keep.tile([P, CHUNK], F32, name=f"y{c}_{t}")
                nc.scalar.activation(y[:], y_ps[:, :CHUNK], ACT.Tanh)
                ys.append(y)
            return ys

        def put(t, c, y):
            nc.vector.tensor_tensor(
                o[t][:].indirect(pos_sb[:, c * CHUNK // 16 : (c + 1) * CHUNK // 16]),
                y[:],
                wgo_sb[:, t * M + c * CHUNK : t * M + (c + 1) * CHUNK],
                ALU.mult,
            )

        def keep_whole(t):
            o.append(late.tile([P, S], F32, name=f"o{t}", align_bytes=64, offset=4096 * t))
            nc.scalar.activation(o[t][:], h[t][:], ACT.Copy, scale=skip_sb[t][:])

        w4_q = quantise("w4", w4_bf)
        x_bf0 = interleave(0, nc.vector.tensor_copy)
        pick(0, 1)
        x_q0 = quantise("x0", x_bf0, codes=late.tile([P, CHUNK], U32, name="x0_codes", align_bytes=64, offset=11776))
        keep_whole(0)
        y0 = second_stage(0, x_q0)
        for t in range(1, PACK):
            pick(t, 1)
            keep_whole(t)
        put(0, 0, y0[0])
        x_bf1 = interleave(1, nc.vector.tensor_copy)
        put(1, 0, y0[1])
        x_q1 = quantise("x1", x_bf1)
        y1 = second_stage(1, x_q1)
        for t in range(2, PACK):
            put(t, 0, y0[t])
        for t in range(PACK):
            put(t, 1, y1[t])
            nc.sync.dma_start(out=dealt(out)[t], in_=o[t][:])
